import numpy as np, ml_dtypes
CORES = [36,164,52,180,100,228,116,244]
N = 8
import mx_ref
BF = ml_dtypes.bfloat16
def gentries(a):
    return np.ascontiguousarray(a.reshape(8, 16, -1).transpose(0, 2, 1)).reshape(8, -1)
def gtable(e):
    e = np.asarray(e); return np.ascontiguousarray(e.reshape(8, -1, 16).transpose(0, 2, 1)).reshape(128, -1).astype(np.int32)
def gcols(t, e):
    v = np.concatenate([t.reshape(8, 16, -1, 4), np.zeros((8, 16, 1, 4), BF)], axis=2)
    return np.ascontiguousarray(np.stack([v[g][:, e[g]] for g in range(8)])).reshape(128, -1)
def tile(rs):
    return np.stack(rs, axis=2).reshape(128, -1).astype(BF)
def pick(q, e):
    c = np.concatenate([q[0].reshape(128, -1, 4), np.zeros((128, 1, 4), np.uint8)], axis=1); s = np.concatenate([q[1], np.ones((16, 1), np.uint8)], axis=1)
    return (np.ascontiguousarray(c[:, e].reshape(128, -1)), np.ascontiguousarray(s[:, e]))
def join(*qs):
    return (np.concatenate([q[0] for q in qs], axis=1), np.concatenate([q[1] for q in qs], axis=1))
def put(q, e, v):
    c, s = q[0].reshape(128, -1, 4).copy(), q[1].copy(); c[:, e] = v[0].reshape(128, -1, 4); s[:, e] = v[1]
    return (c.reshape(128, -1), s)
def pk(c, s):
    return (np.ascontiguousarray(c), mx_ref.live(s))
def emit(q):
    return q[0], q[1]
def packed(v, rng):
    q = [mx_ref.quantize(np.ascontiguousarray(v[r])) for r in range(N)]
    return np.stack([a for a, b in q]), np.stack([mx_ref.plane(b, rng) for a, b in q])
def values_of_codes():
    e, c = np.zeros((128, 128, 4), np.float32), np.zeros((128, 2, 4), np.uint8)
    e[np.arange(128), np.arange(128), 0] = 1
    c[:127, :, 0] = np.arange(256).reshape(2, 128).T[:127]
    return mx_ref.matmul(mx_ref.quantize(e.reshape(128, 512).astype(BF)), (c.reshape(128, 8), np.full((16, 2), 127, np.uint8))).T.reshape(-1).astype(np.float64)
CODE_VALUE, SCALE_VALUE = values_of_codes(), 2.0 ** (np.arange(256) - 127.0)
def decode(q):
    return (CODE_VALUE[q[0]].reshape(16, 8, -1, 4) * SCALE_VALUE[q[1]][:, None, :, None] + 0.0).reshape(128, -1).astype(np.float32)
def f(rng, *shape):
    return mx_ref.flush((rng.standard_normal(shape, dtype=np.float32) * np.exp2(rng.integers(-2, 3, shape[:-1] + (1,)))).astype(BF))
def wide(rng, *shape, cols=0):
    v = rng.standard_normal(shape, dtype=np.float32) * np.exp2(rng.integers(-12, 13, shape)).astype(np.float32)
    if cols: v *= np.repeat(np.exp2(rng.integers(-cols, cols + 1, shape[:-2] + (1, shape[-1] // 4))) * (rng.random(shape[:-2] + (1, shape[-1] // 4)) > 0.0625), 4, axis=-1).astype(np.float32)
    return mx_ref.flush(v.astype(BF))
C, A, R = 352, 288, 3
STEP = [3, 6, 4]
def nearest(s, a, b):
    at = lambda e: np.abs(s - np.take_along_axis(s, e, axis=1))
    return np.where(at(b) < at(a), b, a)
def depths(b):
    k = np.zeros((8, C), int)
    for i in range(1, C): k[:, i] = (k[np.arange(8), b[:, i]] + 1) % 4
    return k
def gput(t, e, h):
    a, b = t.reshape(8, 16, -1, 4).copy(), h.reshape(8, 16, -1, 4)
    for g in range(8): a[g][:, e[g]] = b[g]
    return a.reshape(128, -1)
def big(v):
    v = v.astype(np.float32)
    v[np.abs(v) < np.float32(2.0 ** -16)] = 0
    return v.astype(BF)
def numbers_of(rng):
    return {"x": big(f(rng, N, 128, 4 * C)), "u": np.array(f(rng, N, 128, 512)), "v": np.array(f(rng, N, 128, 512))}
def layers(rng):
    return big(f(rng, N, 128, 2048)).reshape(N, 8, 16, 4, 8, 16, 4)
def weights(rng, w):
    c, p = packed(np.ascontiguousarray(w).reshape(N, 128, 2048), rng)
    return {"wc": c, "ws": p}
def listed(a, b):
    return np.stack([gtable(np.concatenate([a[r], b[r]], axis=1)) for r in range(N)])
def candidates(rng):
    reach = np.stack([np.where(rng.permutation(8) < 4, C, 8) for r in range(N)])[:, :, None]
    n = np.minimum(np.maximum(np.arange(C), 1), reach)
    a, b = [np.maximum(np.arange(C) - 1 - rng.integers(0, n), 0) for k in range(2)]
    return {"cd": listed(a, b)}
def signs(rng):
    return np.stack([rng.permutation(8) % 2 * 2.0 - 1.0 for r in range(N)])
def setup_inputs(rng):
    return {**numbers_of(rng), **weights(rng, layers(rng)), **candidates(rng)}
def setup_inputs_ties(rng):
    d = numbers_of(rng)
    e = rng.permutation(N)
    x = d["x"].reshape(N, 8, 16, C, 4)
    for r in range(N):
        k = np.zeros(C, int) if r == e[0] else rng.permutation(C) % 3
        a = x[r][:, :8, :3].copy()
        a[:, :, 2] = 0
        x[r][:, :8] = a[:, :, k]
    x[e[1]] = 0
    u = d["u"].reshape(N, 8, 16, 128, 4)
    u[:, :, 8:, ::16] = 0
    w = layers(rng)
    w[:, :, :, :, :, :8] = 0
    return {"x": x.reshape(N, 128, 4 * C), "u": u.reshape(N, 128, 512), "v": d["v"], **weights(rng, w), **candidates(rng)}
def setup_inputs_near(rng):
    d = numbers_of(rng)
    x = np.zeros((N, 8, 16, C, 4), np.float32)
    u = d["u"].reshape(N, 128, 128, 4)
    u[:, :, ::16] = 0
    o, c = rng.permutation(N) % 4, signs(rng)
    for r in range(N):
        m = np.full((8, 1), 256)
        m[np.argsort(c[r], kind="stable")[::2]] = 4
        s = rng.integers(0, m, (8, C))
        size = 1.0 if o[r] < 2 else 2.0 ** -7
        g = ((s[:, :, None] >> np.arange(8)) & 1) * np.exp2(np.arange(8) - 23.0) * size
        if o[r] < 3: x[r, :, 0, :, 0] = c[r][:, None] * rng.integers(0, 2, (8, C)) * size
        x[r, :, 8] = g[:, :, :4]
        x[r, :, 9] = g[:, :, 4:]
        x[r, :, 10:] = rng.integers(4, 8, (8, 6, C, 4)) * 2.0 ** -22 * size
        k = 1.0 if o[r] == 0 else 2.0 ** -30
        for h in range(0, 128, 16):
            u[r, h, h, 0] = k
            u[r, h + 8:h + 10, h] = k
    w = layers(rng)
    w[:, :, :10] = 0
    w[:, :, :, :, :, :10] = 0
    return {"x": x.reshape(N, 128, 4 * C).astype(BF), "u": u.reshape(N, 128, 512), "v": d["v"], **weights(rng, w), **candidates(rng)}
def setup_inputs_huge(rng):
    d = numbers_of(rng)
    z = rng.permutation(N) < N // 2
    k = np.stack([rng.choice([-1.0, -0.25] if z[r] else [-1.0, -0.5, 0.5, 1.0], C) for r in range(N)])
    x = 2.0 ** 28 * (0.8 + 0.2 * rng.random((N, 128, C, 4))) * k[:, None, :, None]
    u = d["u"].reshape(N, 128, 128, 4)
    a = 2.0 ** 30 * (1 - 0.25 * rng.random((N, 128, 8, 4))) * signs(rng)[:, None, :, None]
    u[:, :, ::16] = a.astype(np.float32).astype(BF)
    w = np.zeros((N, 128, 4, 128, 4), np.float32)
    i = np.arange(128)
    for b in range(4): w[:, i, b, i, b] = -1
    return {"x": x.astype(np.float32).reshape(N, 128, 4 * C).astype(BF), "u": u.reshape(N, 128, 512), "v": d["v"], **weights(rng, w.astype(BF)), **candidates(rng)}
def shape(rng, k):
    if k == 0: return np.maximum(np.arange(C) - 1, 0)
    if k == 1: return np.zeros(C, int)
    if k == 8:
        b = np.full(C, 1)
        b[:2] = 0
        return b
    if k == 9:
        n = A - 24
        b = np.full(C, 3)
        b[:4] = 0, 0, 1, 2
        b[n + 3:n + 11] = n - 5 + rng.permutation(8)
        b[n + 11:n + 19] = n + 3 + rng.permutation(8)
        b[n + 19:] = n + 11 + rng.integers(0, 8, C - n - 19)
        return b
    n = [C - 3, A, A - 1, A + 1, A - 2, 1][k - 2]
    b = rng.integers(0, 3, C) if k in (3, 4, 5) else np.full(C, 2)
    b[:4] = 0, 0, 1, 2
    b[4 + rng.permutation(C - 4)[:n - 1]] = 3
    return b
def setup_inputs_trees(rng):
    d = setup_inputs(rng)
    m = rng.permutation(10)
    b = np.stack([np.stack([shape(rng, k) for k in rng.permutation(np.delete(np.arange(10), [m[r], m[r - 1]]))]) for r in range(N)])
    d["cd"] = listed(b, b)
    return d
def setup_inputs_spread(rng):
    d = setup_inputs(rng)
    d["x"] = big(wide(rng, N, 128, 4 * C, cols=6))
    return d
def check_inputs(d):
    b = []
    for k in ("x", "u", "v"):
        a = np.abs(d[k].astype(np.float32))
        if not (np.isfinite(a).all() and ((a == 0) | (a >= 2.0 ** -30) & (a <= 2.0 ** 30)).all()): b.append("a value of " + k)
    none, least, most = [emit(mx_ref.quantize(np.full((128, 16), k, np.float32).astype(BF)))[1][0, 0] for k in (0.0, 2.0 ** -30, 2.0 ** 30)]
    for r in range(N):
        if ((d["wc"][r] == 0x7F) | (d["wc"][r] == 0xFF)).any(): b.append("wc: a code that is no number")
        s = mx_ref.live(d["ws"][r])
        if ((s != none) & ((s < least) | (s > most))).any(): b.append("ws: a scale out of range")
        e = gentries(d["cd"][r]).reshape(8, 2, C)
        if ((e < 0) | (e > np.maximum(np.arange(C) - 1, 0))).any(): b.append("cd: a candidate that isn't lower")
    return b
def reference(x, u, v, wc, ws, cd):
    qu = [mx_ref.quantize(u[r]) for r in range(N)]
    lay = [pk(wc[r], ws[r]) for r in range(N)]
    can = [gentries(cd[r]) for r in range(N)]
    now = [x[r] for r in range(N)]
    for t in range(R):
        held, took, depth, base, sent = [], [], [], [], []
        for r in range(N):
            q = mx_ref.quantize(now[r])
            b = nearest(mx_ref.matmul(qu[r], q)[::16], can[r][:, :C], can[r][:, C:])
            k = depths(b)
            o = np.argsort(k, axis=1, kind="stable")[:, :A]
            place = np.zeros((8, C), int)
            np.put_along_axis(place, o, np.arange(A)[None], axis=1)
            k, b = np.take_along_axis(k, o, axis=1), np.take_along_axis(b, o, axis=1)
            h = decode(q).astype(BF)
            p = gcols(h, o).astype(np.float32) - gcols(h, np.where(k > 0, b, -1)).astype(np.float32)
            sent.append(mx_ref.quantize(p.astype(BF)))
            held.append(h)
            took.append(o)
            depth.append(k)
            base.append(np.take_along_axis(place, b, axis=1))
        made = []
        for r in range(N):
            e = (r - STEP[t]) % N
            m = decode(sent[e]).astype(BF)
            for k in (1, 2, 3): m = (m.astype(np.float32) + gcols(m, np.where(depth[e] == k, base[e], -1)).astype(np.float32)).astype(BF)
            q = mx_ref.quantize(m)
            z = gcols(held[r], took[r])
            h = tile([mx_ref.matmul(pick(lay[r], np.arange(128 * b, 128 * b + 128)), q) * np.float32(0.015625) + z[:, b::4].astype(np.float32) for b in range(4)])
            made.append(gput(held[r], took[r], h))
        now = made
    y = np.zeros((N, 128, C), np.float32)
    oc, osc = np.zeros((N, 128, 4 * C), np.uint8), np.zeros((N, 16, C), np.uint8)
    for r in range(N):
        q = mx_ref.quantize(now[r])
        y[r] = mx_ref.matmul(mx_ref.quantize(v[r]), q)
        oc[r], osc[r] = emit(q)
    return {"y": y, "oc": oc, "osc": osc}

from concourse.mybir import dt, AluOpType, ActivationFunctionType

C, A, R, N = 352, 288, 3, 8
STEP = [3, 6, 4]
KW = 131072.0
PW = 296
CODE = "float8_e4m3fn_x4"

SCRATCH = {"psa": ("psum", [128, 2048], "float32"), "psb": ("psum", [128, 2048], "float32")}
for _d, _l in (
        ("bfloat16", (("xt", 4 * C), ("ut", 512), ("vt", 512), ("ones", 528), ("ea", 528), ("nodev", C), ("wmul", C), ("wmin", C),
                      ("l1", 16 + 2 * C), ("l2", 8 + C), ("l4", 8 + C), ("l8", 8 + C), ("l16", 8 + C), ("l32", 8 + C), ("wr", 6 * C),
                      ("wrx", C), ("wro", A), ("xp", 8 + C), ("pa", C), ("pb", C), ("orep", C), ("fown", 4 * C), ("fint", 4 * C),
                      ("fbase", 4 * C), ("pint", 4 * C), ("nsb", 4 * C), ("tmp", 4 * C), ("m0", 4 * C), ("m1", 4 * C), ("m2", 4 * C),
                      ("m3", 4 * C), ("mint", 4 * A))),
        ("float16", (("sd0", 2 * C), ("sd1", 2 * C))),
        ("float32", (("c16", 32), ("kw", 18), ("col", 8), ("w72", 72), ("ssb", C), ("d1", C), ("d2", C), ("g1", C), ("g2", C), ("a1", C),
                     ("a2", C), ("ab", 2 * C), ("abw", 2 * C), ("vv", 44), ("gg", 44), ("hh", 44), ("tf", 8), ("z", 44), ("z2", 22),
                     ("s72", 72), ("o72", 72), ("prod", 4 * PW), ("ysb", C))),
        ("int32", (("cdi", 44), ("i16", 16), ("u16", 16), ("ik", 18), ("ti", 2), ("zi", 22), ("zj", 22))),
        ("uint16", (("cdo", 44), ("upo", 8), ("off", 110), ("offs", 44), ("b4", 88), ("plo", 22), ("plc", 22))
         + tuple((k + str(t), n) for t in range(R) for k, n in (("bw", 22), ("lb", 22), ("fo", 18), ("lf", 18)))),
        (CODE, (("uq", 128), ("upq", 128), ("vq", 128), ("wq", 512), ("eq", 512), ("rq", C), ("bq", C), ("nq", C), ("mq", A))
         + tuple(("tq" + str(t), C) for t in range(R + 1)) + tuple(("lq" + str(t), C) for t in range(R))),
        ("uint8", (("us", 128), ("ups", 128), ("vs", 128), ("wp", 512), ("es", 512), ("rs", C), ("bs", C), ("ns", C), ("ms", A))
         + tuple(("tp" + str(t), C) for t in range(R + 1)) + tuple(("lp" + str(t), C) for t in range(R)))):
    for _k, _n in _l:
        SCRATCH[_k] = ("sbuf", [128, _n], _d)

SEMAPHORES = (["sV", "sS", "sP", "sG", "sent", "dcd", "dx0", "dx1", "du", "dv", "dwc", "dws", "doc", "dos", "dy"]
              + ["a%s%d" % (k, t) for k in "tbf" for t in range(R)])

PLAN = {
    "parts": ((0, 192), (192, C)),
    "mparts": ((0, 160), (160, A)),
    "assist": "0011",
}
CY, GA, SCA, LAT, RLAT, BIG = 1.04e-3, 1.56, 3.8, 0.06, 2.3, 5.0

ORDER = {
    "V": "53 14 46 54 13 10 17 16 15 52 51 48 55 50 18 24 56 12 57 22 20 49 23 21 29 44 26 37 65 40 43 75 76 66 41 79 80 47 81 83 88 89 108 45 109 92 93 114 94 96 115 110 82 111 112 120 121 95 117 118 59 126 127 123 124 42 132 62 133 186 129 187 130 188 134 58 135 191 136 19 192 63 193 140 25 145 155 199 200 203 152 202 201 149 204 209 146 207 208 205 210 206 214 60 154 157 148 215 212 151 216 167 217 166 218 211 219 213 224 223 225 226 222 221 227 228 61 234 232 231 236 238 237 242 240 246 259 247 260 220 264 270 271 272 269 273 277 275 276 274 "
         "287 288 278 291 292 293 295 300 301 320 321 304 305 326 306 327 308 331 323 324 307 332 333 294 329 330 338 339 335 336 344 345 341 399 342 400 346 347 403 348 404 405 352 357 358 411 367 412 364 415 413 361 420 369 360 414 419 421 417 422 416 366 426 418 363 427 379 428 424 429 378 430 431 423 436 434 425 437 433 438 435 439 440 446 64 444 443 448 450 452 449 454 455 458 459 472 432 482 483 484 481 485 489 486 488 487 "
         "499 500 490 503 509 504 505 507 512 513 532 533 506 516 538 517 518 539 520 543 519 535 536 544 545 541 542 550 551 547 548 556 557 553 610 554 611 558 559 614 560 615 616 564 576 569 579 621 573 624 570 632 623 625 626 627 631 581 633 628 634 629 635 638 578 630 572 639 575 640 591 641 590 636 642 637 643 647 648 646 649 645 650 651 652 658 656 655 660 662 661 666 664 670 683 671 684 675 644 694 698 695 699 697 700 693 696 704 701 703",
    "S": "3 0 32 33 34 35 36 27 28 39 38 30 31 72 73 74 77 78 85 86 87 107 90 91 113 106 119 116 125 122 131 128 142 189 190 144 138 194 195 196 197 198 156 153 147 150 104 102 100 163 161 159 183 165 176 181 233 173 179 170 235 239 241 257 244 243 256 245 258 251 266 253 268 255 249 262 "
         "284 285 286 289 290 297 298 299 319 302 303 325 318 322 328 337 334 343 340 398 354 401 402 356 350 406 407 408 409 410 368 359 365 362 316 314 312 375 377 373 371 393 388 445 395 385 391 382 447 451 453 456 469 470 457 471 468 463 476 478 465 467 480 461 474 "
         "496 497 498 501 502 530 510 511 531 514 515 537 534 540 549 546 555 552 566 612 613 568 562 617 618 619 620 622 580 571 577 526 574 528 524 589 587 583 585 605 600 607 657 597 603 594 659 663 665 668 681 667 680 669 682 688 690 677 686 673 692 679 706 712",
    "P": "71 84 103 105 101 141 137 143 99 139 164 162 160 158 182 174 175 184 180 177 168 171 185 172 178 169 250 263 265 267 252 254 248 261 283 296 315 317 313 353 351 311 355 349 376 374 372 370 394 396 386 392 387 380 383 384 381 397 389 390 462 466 475 477 479 464 473 460 "
         "495 529 508 527 523 565 561 567 563 588 525 584 586 582 604 606 598 601 599 592 608 595 596 602 609 593 674 687 676 672 689 685 691 678 705 702",
    "G": "7 9 8 11 67 68 69 97 229 279 281 280 309 441 491 493 492 521 653",
    "Y": "1 2 6 5 4 710 708 709 711 707",
    "arr": "70 98 230 282 310 442 494 522 654",
}


def rank_program(g, core, T, topo):
    rank = T.rank_of(core)
    if rank is None:
        return
    Q = {"V": g.vector, "S": g.scalar, "P": g.tensor, "G": g, "Y": g.sync}
    AL, AF = AluOpType, ActivationFunctionType
    ops, last_w, readers = [], {}, {}

    def op(q, fn, reads, writes, cost, sem=None, inc=1, later=0.0, after=()):
        deps = set()
        for k in reads:
            if k in last_w:
                deps.add(last_w[k])
        for k in writes:
            if k in last_w:
                deps.add(last_w[k])
            deps.update(readers.get(k, []))
        ops.append({"q": q, "fn": fn, "deps": deps, "after": set(after), "src": sem if sem else "s" + q, "sig": bool(sem), "inc": inc,
                    "cost": cost, "later": later})
        me = len(ops) - 1
        for k in reads:
            readers.setdefault(k, []).append(me)
        for k in writes:
            last_w[k] = me
            readers[k] = []
        return me

    V, S = g.vector, g.scalar
    u8, u32 = dt.uint8, dt.uint32

    def cy(n):
        return max(64, n) * CY

    def ga(n):
        return 0.06 + n * GA * CY

    def ts(out, in0, s1, s2, op0, op1, r, w):
        if op1 is None:
            op("V", lambda: V.tensor_scalar(out, in0, s1, None, op0), r, w, cy(0))
        else:
            op("V", lambda: V.tensor_scalar(out, in0, s1, s2, op0, op1), r, w, cy(0))

    def tt(out, a, b, o, r, w, c):
        op("V", lambda: V.tensor_tensor(out, a, b, o), r, w, c)

    def ms(ap, k, w, n=0):
        op("V", lambda: V.memset(ap, k), (), w, cy(n))

    def scan(out, a, b, init, o0, o1, r, w, c):
        op("V", lambda: V.tensor_tensor_scan(out, a, b, init, o0, o1), r, w, c)

    def act(out, a, r, w, c, func):
        op("S", lambda: S.activation(out, a, func), r, w, c)

    def vcp(out, a, r, w, c):
        op("V", lambda: V.tensor_copy(out, a), r, w, c)

    def cp(out, a, r, w, c, scale=None):
        fv = (lambda: V.tensor_copy(out, a)) if scale is None else (lambda: V.tensor_scalar(out, a, scale, None, AL.mult))
        fs = (lambda: S.activation(out, a, AF.Copy)) if scale is None else (lambda: S.activation(out, a, AF.Copy, scale=scale))
        ops[op("S", fs, r, w, c)]["alt"] = {"V": (fv, c), "S": (fs, c)}

    def qz(q, s, a, r, w, n):
        op("V", lambda: V.quantize_mx(q, s, a), r, w, 0.015 + 1.1e-3 * n)

    def bank(b, a0, a1):
        return (T.psa if b < 4 else T.psb)[:, 512 * (b % 4) + a0:512 * (b % 4) + a1]

    def mm(b, n, lq, ls, rq, rs, r, first=True, last=True):
        op("P", lambda: g.tensor.matmul_mx(bank(b, 0, n), lq, ls, rq, rs, first, last), r, [("ps", b)], (n + 16) * 0.65e-3)

    def decode(b, bk, q, s, keys, first=True, last=True):
        mm(bk, C, T.eq[:, 128 * b:128 * b + 128], T.es[:, 128 * b:128 * b + 128], q[:], s[:], keys + [("e", b)], first, last)

    def dma(q, out, in_, sem, r, w, later):
        op(q, lambda: Q[q].dma_start(out, in_), r, w, 0.1, sem=sem, inc=16, later=later)

    sent = [0]

    def send(dst, out, in_, rsem, r):
        rid, pid = topo.addr(dst, core)
        m = topo.mask(core, dst)
        sent[0] += len(topo.engines(core, dst))
        return op("G", lambda: g.remote_dma(out, in_, T.sem[rsem], T.sem.sent, pid, rid, m), r, (), 0.3)

    def arrival(sem, src, mine, w, later):
        op("arr", None, (), w, 0.0, sem=sem, inc=len(mine) * len(topo.engines(src, core)), later=later, after=mine)

    def plane(buf, t, n=C):
        return buf[:, n * t:n * (t + 1)]

    parts, mparts = PLAN["parts"], PLAN["mparts"]

    def X(a):
        return [("x", b, a) for b in range(4)]

    dma("S", T.cdi[:], T.cd[:], "dcd", (), ["cdi"], 2.0)
    for i, (a, e) in enumerate(parts):
        dma("Y", T.xt[:, 4 * a:4 * e], T.x[:, 4 * a:4 * e], "dx%d" % i, (), X(a), 3.2 + i)
    dma("S", T.ut[:], T.u[:], "du", (), ["ut"], 2.6)
    dma("Y", T.wq[:].bitcast(u8), T.wc[:], "dwc", X(parts[-1][0]), ["wq"], 4.0)
    dma("Y", T.wp[:], T.ws[:], "dws", X(parts[-1][0]), ["wp"], 4.0)
    dma("Y", T.vt[:], T.v[:], "dv", X(parts[-1][0]), ["vt"], 4.0)

    op("G", lambda: g.iota(T.i16[:], [[1, 16]], 128, -1), (), ["i16"], 0.17)
    op("G", lambda: g.iota(T.ik[:], [[16, 18]], 0, 0), (), ["ik"], 0.17)
    op("G", lambda: g.iota(T.nodev[:], [[1, C]], -172, 0, allow_small_or_imprecise_dtypes=True), (), ["nodev"], 0.86)
    ms(T.ones[:], 1.0, ["ones"], 264)
    op("G", lambda: g.affine_select(T.ea[:], T.ones[:], [[-1, 528]], AL.is_equal, 0.0, 3, 4), ["ones"], ["ea"], 1.27)
    vcp(T.upo[:], T.ik[:, 0:8], ["ik"], ["upo"], cy(0))
    ts(T.u16[:], T.i16[:], 15, None, AL.bitwise_and, None, ["i16"], ["u16"])
    ms(T.sd0[:, 0:2 * C:2], 0.0, ["sd0e"], 176)
    ts(T.c16[:, 0:16], T.u16[:], 0.0, None, AL.not_equal, None, ["u16"], ["c16a"])
    ts(T.c16[:, 16:32], T.u16[:], 1.0, KW - 1.0, AL.is_equal, AL.mult, ["u16"], ["c16b"])
    ts(T.wmin[:, 0:16], T.u16[:], 0.0, 1048576.0, AL.is_equal, AL.mult, ["u16"], ["wmin"])
    ts(T.col[:, 3:4], T.u16[:, 15:16], 0.0, 1.0 - 1.0 / KW, AL.is_equal, AL.mult, ["u16"], ["col3"])
    ts(T.col[:, 4:5], T.u16[:, 15:16], -1.0, 15.0, AL.mult, AL.add, ["u16"], ["col4"])
    tt(T.wmul[:, 0:16], T.c16[:, 0:16], T.c16[:, 16:32], AL.add, ["c16a", "c16b"], ["wmul"], cy(0))
    vcp(T.cdo[:], T.cdi[:], ["cdi"], ["cdo"], cy(0))
    ts(T.col[:, 0:1], T.col[:, 3:4], 1.0 / KW, None, AL.add, None, ["col3"], ["col"])
    ts(T.col[:, 1:2], T.col[:, 3:4], 1.0 / KW, -1.0, AL.add, AL.mult, ["col3"], ["col1"])
    ts(T.col[:, 2:3], T.col[:, 3:4], 1.0 / KW, 2.0, AL.add, AL.mult, ["col3"], ["col2"])
    ts(T.kw[:], T.ik[:], T.col[:, 4:5], None, AL.add, None, ["ik", "col4"], ["kw"])
    qz(T.uq[:], T.us[:], T.ut[:], ["ut"], ["uq"], 128)
    for buf, nm in ((T.wmul, "wmul"), (T.wmin, "wmin")):
        n = 16
        while n < C:
            cp(buf[:, n:min(2 * n, C)], buf[:, 0:min(n, C - n)], [nm], [nm], cy(n))
            n *= 2
    vcp(T.upq[:].bitcast(u32), T.uq[:].bitcast(u32).indirect(T.upo[:, 0:8]), ["uq", "upo"], ["upq"], ga(128))
    cp(T.ups[:], T.us[:].indirect(T.upo[:, 0:8]), ["uq", "upo"], ["ups"], ga(128))
    cp(T.sd1[:, 1:2 * C:2], T.nodev[:].indirect(T.cdo[:, 0:22]), ["nodev", "cdo"], ["sd1a"], ga(C))
    tt(T.sd0[:, 1:2 * C:2], T.nodev[:].indirect(T.cdo[:, 22:44]), T.sd1[:, 1:2 * C:2], AL.subtract, ["nodev", "cdo", "sd1a"], ["sd0"], ga(C))
    ms(T.sd1[:, 1:2], -177.0, ["sd1a"])
    for b in range(4):
        qz(T.eq[:, 128 * b:128 * b + 128], T.es[:, 128 * b:128 * b + 128], T.ea[:, 3 - b:515 - b], ["ea"], [("e", b)], 128)
    ms(T.l1[:, 0:16], -177.0, ["l1v"])
    ts(T.l1[:, 3:8:2], T.ik[:, 0:3], 0.0625, -180.0, AL.mult, AL.add, ["ik"], ["l1v"])
    for buf, nm in ((T.l4, "l4"), (T.l8, "l8"), (T.l16, "l16")):
        ts(buf[:, 0:8], T.ik[:, 0:8], 0.0625, -180.0, AL.mult, AL.add, ["ik"], [nm + "v"])
    ts(T.l2[:, 2:8], T.ik[:, 0:6], 0.0625, -180.0, AL.mult, AL.add, ["ik"], ["l2v"])
    ts(T.l2[:, 0:2], T.ik[:, 2:4], 0.0625, -180.0, AL.mult, AL.add, ["ik"], ["l2u"])
    ms(T.xp[:, 0:8], 1.0, ["xpv"])
    for d, c in ((1, -1.0), (2, 512.0), (3, -512.0)):
        ms(T.xp[:, d:d + 1], c, ["xpv"])
    ms(T.w72[:], 1.0, ["w72"])
    for b in range(4):
        ms(T.prod[:, PW * b + A:PW * b + PW], 0.0, [("prz", b)])
    ms(T.w72[:, 0:72:4], 0.0, ["w72"])
    ms(T.w72[:, 3:72:4], float(C), ["w72"])
    qz(T.vq[:], T.vs[:], T.vt[:], ["vt"], ["vq"], 128)

    M = [T.m0, T.m1, T.m2, T.m3]

    def upto(name, e):
        return [(name, a) for a, b in parts if a < e]

    def over(name, a0, e0):
        return [(name, a) for a, b in parts if a < e0 and b > a0]

    def relu(buf, src, sg, r, w):
        fs = lambda: S.activation(buf, src, AF.Relu, scale=sg)
        fv = lambda: V.tensor_scalar(buf, src, sg, 0.0, AL.mult, AL.max)
        ops[op("S", fs, r, w, cy(C))]["alt"] = {"S": (fs, cy(C)), "V": (fv, cy(C // 2))}

    for t in range(R):
        dst = T.cores[(rank + STEP[t]) % N]
        src = T.cores[(rank - STEP[t]) % N]
        tq, tp, lq, lp = T["tq%d" % t], T["tp%d" % t], T["lq%d" % t], T["lp%d" % t]
        bw, lb, fo, lf = T["bw%d" % t], T["lb%d" % t], T["fo%d" % t], T["lf%d" % t]
        kt, kl, kb, kf, kw = "tq%d" % t, "lq%d" % t, "lb%d" % t, "lf%d" % t, "bw%d" % t
        KT = upto(kt, C)

        for a, e in parts:
            qz(tq[:, a:e], tp[:, a:e], T.xt[:, 4 * a:4 * e], X(a), [(kt, a)], e - a)
        sn = [send(dst, lq[:, a:e].bitcast(u8), tq[:, a:e].bitcast(u8), "at%d" % t, [(kt, a)]) for a, e in parts]
        sn.append(send(dst, lp[:], tp[:], "at%d" % t, KT))
        arrival("at%d" % t, src, sn, [kl], BIG - 0.8)

        for i, (a, e) in enumerate(parts):
            n, c0, c1 = e - a, a // 16, e // 16
            mm(i, n, T.upq[:], T.ups[:], tq[:, a:e], tp[:, a:e], [(kt, a), "upq", "ups"])
            cp(T.ssb[:, a:e], bank(i, 0, n), (), [("ps", i), ("ssb", a)], cy(n))
            SS = upto("ssb", e) + ["cdo"]
            cp(T.g1[:, a:e], bank(i, 0, n), (), [("ps", i), ("g1", a)], cy(n))
            cp(T.g2[:, a:e], T.ssb[:, 0:e].indirect(T.cdo[:, 22 + c0:22 + c1]), SS, [("g2", a)], ga(n))
            tt(T.d1[:, a:e], T.ssb[:, 0:e].indirect(T.cdo[:, c0:c1]), T.g1[:, a:e], AL.subtract, SS + [("g1", a)], [("d1", a)], ga(n))
            tt(T.d2[:, a:e], T.g2[:, a:e], bank(i, 0, n), AL.subtract, [("g2", a)], [("ps", i), ("d2", a)], cy(n))
            act(T.a1[:, a:e], T.d1[:, a:e], [("d1", a)], [("a1", a)], cy(n), AF.Abs)
            act(T.a2[:, a:e], T.d2[:, a:e], [("d2", a)], [("a2", a)], cy(n), AF.Abs)
            tt(T.sd1[:, 2 * a:2 * e:2], T.a2[:, a:e], T.a1[:, a:e], AL.is_lt, [("a2", a), ("a1", a)], [("sd1", a)], cy(2 * n))
            scan(T.l1[:, 16 + 2 * a:16 + 2 * e], T.sd0[:, 2 * a:2 * e], T.sd1[:, 2 * a:2 * e], 0.0, AL.mult, AL.add,
                 ["sd0", "sd0e", "sd1a", ("sd1", a)], [("l1", a)], cy(n))
            scan(T.wr[:, a:e], T.wmul[:, a:e], T.l1[:, 17 + 2 * a:16 + 2 * e:2], 0.0, AL.mult, AL.add, ["wmul", ("l1", a)], [("wr0", a)], cy(n // 2))
            ts(bw[:, c0:c1], T.wr[:, a + 15:e:16], T.col[:, 0:1], 172.25, AL.mult, AL.add, [("wr0", a), "col"], [(kw, a)])
            ts(T.off[:, c0:c1], T.wr[:, a + 15:e:16], T.col[:, 2:3], 361.25, AL.mult, AL.add, [("wr0", a), "col2"], [("off0", a)])
        arrival("ab%d" % t, src, [send(dst, lb[:], bw[:], "ab%d" % t, upto(kw, C))], [kb], RLAT)
        for b in range(4):
            decode(b, 4 + b, tq, tp, KT)
            cp(plane(T.fown, b), bank(4 + b, 0, C), (), [("ps", 4 + b), ("fown", b)], cy(C))

        lv = [(T.l1, "l1", ["l1v"]), (T.l2, "l2", ["l2v", "l2u"]), (T.l4, "l4", ["l4v"]), (T.l8, "l8", ["l8v"]), (T.l16, "l16", ["l16v"]), (T.l32, "l32", [])]
        for k in range(5):
            for a, e in parts:
                n, c0, c1 = e - a, a // 16, e // 16
                win = T.l1[:, 0:16 + 2 * e] if k == 0 else lv[k][0][:, 0:8 + e]
                nm, wn = lv[k + 1][1], "wr%d" % (k + 1)
                cp(lv[k + 1][0][:, 8 + a:8 + e], win.indirect(T.off[:, 22 * k + c0:22 * k + c1]),
                   upto(lv[k][1], e) + lv[k][2] + over("off%d" % k, a, e), [(nm, a)], ga(n))
                w0 = C * (k + 1)
                scan(T.wr[:, w0 + a:w0 + e], T.wmul[:, a:e], lv[k + 1][0][:, 8 + a:8 + e], 0.0, AL.mult, AL.add, ["wmul", (nm, a)], [(wn, a)], cy(n // 2))
                out = T.off[:, 22 * (k + 1) + c0:22 * (k + 1) + c1] if k < 4 else T.offs[:, c0:c1]
                ts(out, T.wr[:, w0 + a + 15:w0 + e:16], T.col[:, 0:1], 180.25, AL.mult, AL.add, [(wn, a), "col"], [("off%d" % (k + 1), a)])

        for b in range(4):
            decode(b, b, lq, lp, [kl])
            cp(T.fint[:, b:4 * C:4], bank(b, 0, C), (), [("ps", b), ("fint", b)], cy(C))
        FI = [("fint", b) for b in range(4)]
        qz(T.rq[:], T.rs[:], T.fint[:], FI, ["rq"], C)
        for b in range(4):
            ts(T.b4[:, 22 * b:22 * b + 22], lb[:], 4.0, float(b), AL.mult, AL.add, [kb], [("b4", b)])
            cp(T.fbase[:, b:4 * C:4], T.fint[:].indirect(T.b4[:, 22 * b:22 * b + 22]), FI + [("b4", b)], [("fbase", b)], ga(C))
            tt(T.pint[:, b:4 * C:4], bank(b, 0, C), T.fbase[:, b:4 * C:4], AL.subtract, [("fbase", b)], [("ps", b), ("pint", b)], cy(C))
        for b in range(4):
            decode(b, 4 + b, T.rq, T.rs, ["rq"])
            cp(plane(M[b], 0), bank(4 + b, 0, C), (), [("ps", 4 + b), ("m", b, 0)], cy(C))
        qz(T.bq[:], T.bs[:], T.fbase[:], [("fbase", b) for b in range(4)], ["bq"], C)
        qz(T.nq[:], T.ns[:], T.pint[:], [("pint", b) for b in range(4)], ["nq"], C)
        for b in range(4):
            decode(b, 4 + b, T.bq, T.bs, ["bq"], True, False)
            decode(b, 4 + b, T.nq, T.ns, ["nq"], False, True)
            cp(plane(M[b], 1), bank(4 + b, 0, C), (), [("ps", 4 + b), ("m", b, 1)], cy(C))
        for b in range(4):
            decode(b, b, T.nq, T.ns, ["nq"])
            if PLAN["assist"][b] == "0":
                cp(plane(T.nsb, b), bank(b, 0, C), (), [("ps", b), ("nsb", b)], cy(C))

        for c in range(11):
            cp(T.xp[:, 8 + 32 * c:40 + 32 * c], T.xp[:, 0:8 + 32 * c].indirect(T.offs[:, 2 * c:2 * c + 2]),
               ["xpv"] + over("off5", 32 * c, 32 * c + 32), ["xp"], ga(32))
        xp = T.xp[:, 8:8 + C]
        relu(T.pa[:], xp, 1.0, ["xp"], ["pa"])
        relu(T.pb[:], xp, -1.0, ["xp"], ["pb"])

        scan(T.wrx[:], T.wmul[:], xp, 0.0, AL.mult, AL.add, ["wmul", "xp"], ["wrx"], cy(C // 2))
        scan(T.ab[:, 0:C], T.ones[:, 0:C], T.pa[:], 0.0, AL.mult, AL.add, ["ones", "pa"], ["aba"], cy(C))
        scan(T.ab[:, C:2 * C], T.ones[:, 0:C], T.pb[:], T.ab[:, C - 1:C], AL.mult, AL.add, ["ones", "pb", "aba"], ["abb"], cy(C))
        ts(T.vv[:, 0:22], T.wrx[:, 15:C:16], T.col[:, 0:1], None, AL.mult, None, ["wrx", "col"], ["vva"])
        ts(T.vv[:, 22:44], T.wrx[:, 15:C:16], T.col[:, 1:2], None, AL.mult, None, ["wrx", "col1"], ["vvb"])
        ts(T.gg[:], T.vv[:], 0.0, None, AL.is_gt, None, ["vva", "vvb"], ["gg"])
        ts(T.hh[:], T.vv[:], 2.0, -511.0 / 512.0, AL.is_gt, AL.mult, ["vva", "vvb"], ["hh"])
        tt(T.gg[:], T.gg[:], T.hh[:], AL.add, ["hh"], ["gg"], cy(88))
        ts(T.ti[:], T.ab[:, C - 1:2 * C:C], 1.0 / 512.0, -0.345, AL.mult, AL.add, ["aba", "abb"], ["ti"])
        scan(T.abw[:, 0:C], T.wmin[:], T.ab[:, 0:C], 0.0, AL.add, AL.min, ["wmin", "aba"], ["abwa"], cy(C))
        scan(T.abw[:, C:2 * C], T.wmin[:], T.ab[:, C:2 * C], 0.0, AL.add, AL.min, ["wmin", "abb"], ["abwb"], cy(C))
        ts(T.tf[:, 4:5], T.ti[:, 1:2], -512.0, 512.0 * C, AL.mult, AL.add, ["ti"], ["tf4"])
        ts(T.tf[:, 0:1], T.ti[:, 0:1], -512.0, T.ab[:, C - 1:C], AL.mult, AL.add, ["ti", "aba"], ["tf0"])
        ts(T.tf[:, 1:2], T.ti[:, 1:2], -1.0, float(C), AL.mult, AL.add, ["ti"], ["tf1"])
        ts(T.tf[:, 2:3], T.ti[:, 0:1], T.tf[:, 1:2], None, AL.add, None, ["ti", "tf1"], ["tf2"])
        ts(T.z[:], T.abw[:, 15:2 * C:16], T.tf[:, 4:5], None, AL.add, None, ["abwa", "abwb", "tf4"], ["z"])
        tt(T.z[:], T.z[:], T.gg[:], AL.mult, ["gg"], ["z"], cy(88))
        tt(T.z2[:], T.z[:, 0:22], T.z[:, 22:44], AL.add, ["z"], ["z2"], cy(0))
        ts(T.zi[:], T.z2[:], -1.345, None, AL.add, None, ["z2"], ["zi"])
        ts(T.zj[:], T.zi[:], 511, None, AL.bitwise_and, None, ["zi"], ["zj"])
        vcp(T.plo[:], T.zj[:], ["zj"], ["plo"], cy(0))
        ts(T.plc[:], T.zj[:], float(A), None, AL.min, None, ["zj"], ["plc"])
        for j in range(3):
            ts(T.s72[:, j:72:4], T.kw[:], T.tf[:, j:j + 1], None, AL.is_ge, None, ["kw", "tf%d" % j], [("s72", j)])
        vcp(T.orep[:].indirect(T.plo[:]), T.nodev[:], ["plo", "nodev"], ["orep"], 0.05 + C * SCA * CY)
        scan(T.wro[:], T.wmul[:, 0:A], T.orep[:, 0:A], 0.0, AL.mult, AL.add, ["wmul", "orep"], ["wro"], cy(A // 2))
        ts(T.s72[:, 3:72:4], T.wro[:, 15:A:16], T.col[:, 0:1], None, AL.mult, None, ["wro", "col"], [("s72", 3)])
        scan(T.o72[:], T.w72[:], T.s72[:], 0.0, AL.mult, AL.add, ["w72"] + [("s72", j) for j in range(4)], ["o72"], cy(72))
        ts(fo[:], T.o72[:, 3:72:4], 172.25, None, AL.add, None, ["o72"], ["fo%d" % t])
        arrival("af%d" % t, src, [send(dst, lf[:], fo[:], "af%d" % t, ["fo%d" % t])], [kf], RLAT)

        for j in (2, 3):
            for b in range(4):
                win = plane(M[b], j - 1).indirect(lb[:])
                if PLAN["assist"][b] == "1":
                    cp(plane(T.tmp, b), win, [("m", b, j - 1), kb], [("tmp", b)], ga(C))
                    tt(plane(M[b], j), plane(T.tmp, b), bank(b, 0, C), AL.add, [("tmp", b)], [("ps", b), ("m", b, j)], cy(C))
                else:
                    tt(plane(M[b], j), win, plane(T.nsb, b), AL.add, [("m", b, j - 1), kb, ("nsb", b)], [("m", b, j)], ga(C))
        for i, (a, e) in enumerate(mparts):
            for b in range(4):
                cp(T.mint[:, 4 * a + b:4 * e:4], M[b][:].indirect(lf[:, a // 16:e // 16]), [kf] + [("m", b, j) for j in range(4)], [("mint", b, a)], ga(e - a))
            qz(T.mq[:, a:e], T.ms[:, a:e], T.mint[:, 4 * a:4 * e], [("mint", b, a) for b in range(4)], [("mq", a)], e - a)
            for b in range(4):
                bk = 4 + b - 4 * i
                mm(bk, e - a, T.wq[:, 128 * b:128 * b + 128], T.wp[:, 128 * b:128 * b + 128], T.mq[:, a:e], T.ms[:, a:e], [("mq", a), "wq", "wp"])
                cp(T.prod[:, PW * b + a:PW * b + e], bank(bk, 0, e - a), (), [("ps", bk), ("prod", b, a)], cy(e - a), scale=0.015625)
        for a, e in parts:
            for b in range(4):
                tt(T.xt[:, 4 * a + b:4 * e:4], plane(T.prod, b, PW).indirect(T.plc[:, a // 16:e // 16]), T.fown[:, C * b + a:C * b + e], AL.add,
                   [("prod", b, k) for k, _ in mparts] + [("prz", b), "plc", ("fown", b)], [("x", b, a)], ga(e - a))

    tq, tp = T["tq%d" % R], T["tp%d" % R]
    for i, (a, e) in enumerate(parts):
        qz(tq[:, a:e], tp[:, a:e], T.xt[:, 4 * a:4 * e], X(a), [("tqf", a)], e - a)
        mm(i, e - a, T.vq[:], T.vs[:], tq[:, a:e], tp[:, a:e], [("tqf", a), "vq"])
        cp(T.ysb[:, a:e], bank(i, 0, e - a), (), [("ps", i), ("ysb", a)], cy(e - a))
    KT = upto("tqf", C)
    dma("Y", T.oc[:], tq[:].bitcast(u8), "doc", KT, ["oc"], 2.5)
    for k in range(4):
        dma("Y", T.osc[4 * k:4 * k + 4, :], tp[32 * k:32 * k + 4, :], "dos", KT, [("osc", k)], 2.0)
    dma("S", T.y[:], T.ysb[:], "dy", upto("ysb", C), ["y"], 2.5)

    lines = {q: [int(k) for k in l.split()] for q, l in ORDER.items()}
    for q, l in lines.items():
        for i in l:
            if "alt" in ops[i]:
                ops[i].update(q=q, src="s" + q, fn=ops[i]["alt"][q][0])
            assert ops[i]["q"] == q
    assert sorted(i for l in lines.values() for i in l) == list(range(len(ops)))
    order, done, head = [], set(), {q: 0 for q in lines}
    while len(order) < len(ops):
        before = len(order)
        for q, l in lines.items():
            while head[q] < len(l) and (ops[l[head[q]]]["deps"] | ops[l[head[q]]]["after"]) <= done:
                order.append(l[head[q]])
                done.add(l[head[q]])
                head[q] += 1
        assert len(order) > before

    clock, seq = {}, {}
    for at, i in enumerate(order):
        o = ops[i]
        ck = clock.setdefault(o["q"], {})
        o["waits"] = []
        for d in sorted(o["deps"], key=lambda d: -ops[d]["at"]):
            p = ops[d]
            if ck.get(p["src"], -1) >= p["n"]:
                continue
            o["waits"].append(d)
            p["sig"] = True
            ck[p["src"]] = p["n"]
            for s, k in p["ck"].items():
                if ck.get(s, -1) < k:
                    ck[s] = k
        seq[o["src"]] = seq.get(o["src"], -1) + 1
        o["n"], o["at"], o["ck"] = seq[o["src"]], at, ({} if o["q"] == "arr" else dict(ck))
    count = {}
    for i in order:
        o = ops[i]
        if o["sig"]:
            count[o["src"]] = count.get(o["src"], 0) + o["inc"]
        o["val"] = count.get(o["src"], 0)
    for i in order:
        o = ops[i]
        if o["q"] == "arr":
            continue
        for d in o["waits"]:
            Q[o["q"]].wait_ge(T.sem[ops[d]["src"]], ops[d]["val"])
        ins = o["fn"]()
        if o["sig"]:
            ins.then_inc(T.sem[o["src"]], o["inc"])
    for s in ("doc", "dos", "dy"):
        g.wait_ge(T.sem[s], count[s])
    g.wait_ge(T.sem.sent, sent[0])
